import numpy as np
import ml_dtypes


def mxq(x, axis, fmt="e4m3"):
    dtype, down = {"e4m3": (ml_dtypes.float8_e4m3fn, 7), "e5m2": (ml_dtypes.float8_e5m2, 14)}[fmt]
    v = np.moveaxis(np.asarray(x, np.float32).astype(ml_dtypes.bfloat16).astype(np.float64), axis, -1)
    blocks = v.reshape(v.shape[:-1] + (-1, 32))
    amax = np.abs(blocks).max(-1, keepdims=True)
    byte = np.maximum(np.where(amax > 0, np.frexp(amax)[1] - 1 + 127, 0) - down, 1)
    scale = np.exp2(byte - 127.0)
    codes = (blocks / scale).astype(np.float32).astype(dtype).astype(np.float64)
    return np.moveaxis((codes * scale).reshape(v.shape), -1, axis)


WIDE = False


def mx_kscale(k):
    if not WIDE:
        return np.ones(k)
    levels = np.array([10, -10, 5, -5, 0])
    if k % 512:
        return np.exp2(np.random.permutation(np.resize(levels, k // 32))).repeat(32)
    a = np.empty((k // 512, 16))
    for p in range(k // 512):
        a[p, :8] = np.random.permutation(np.resize(levels, 8))
        for g in range(8):
            far = levels[np.abs(levels - a[p, g]) >= 10]
            a[p, g + 8] = far[np.random.randint(len(far))]
    return np.exp2(a.ravel()).repeat(32)


def f64(x):
    return np.asarray(x).astype(np.float64)


def striped(idx):
    return np.tile(np.asarray(idx).reshape(-1, 16).T, (8, 1)).astype(np.uint16)


def unstriped(offs):
    return offs[:16].T.reshape(-1).astype(np.int64)


E2M1 = np.array([0.0, 0.5, 1.0, 1.5, 2.0, 3.0, 4.0, 6.0, -0.0, -0.5, -1.0, -1.5, -2.0, -3.0, -4.0, -6.0])


def pack_weight(w, fmt):
    k, n = w.shape
    w = f64(np.asarray(w, np.float32).astype(ml_dtypes.bfloat16)).reshape(k // 32, 32, n)
    amax = np.abs(w).max(1)
    if fmt == "e4m3":
        byte = np.frexp(amax)[1] - 1 + 127 - 7
    else:
        mant, ex = np.frexp(amax / 6.0)
        byte = np.where(mant > 0.5, ex, ex - 1) + 127
    byte = np.clip(np.where(amax > 0, byte, 1), 1, 254)
    scaled = (w * np.exp2(127.0 - byte)[:, None, :]).reshape(k, n).astype(np.float32)
    by_word = np.ascontiguousarray(scaled.reshape(k // 512, 128, 4, n).transpose(0, 1, 3, 2))
    if fmt == "e4m3":
        words = by_word.astype(ml_dtypes.float8_e4m3fn).view(np.uint8)
    else:
        c = by_word.astype(ml_dtypes.float4_e2m1fn).view(np.uint8) & 0xF
        words = (c[..., 0::2] | (c[..., 1::2] << 4)).reshape(k // 512, 128, 2 * n)
    return np.ascontiguousarray(words), np.ascontiguousarray(byte.astype(np.uint8).reshape(k // 512, 16, n))


def unpack_weight(words, scales, fmt):
    g, _, n = scales.shape
    words = np.ascontiguousarray(words).reshape(g, 128, n, -1)
    if fmt == "e4m3":
        vals = words.view(ml_dtypes.float8_e4m3fn).astype(np.float64)
    else:
        nib = np.empty((g, 128, n, 4), np.uint8)
        nib[..., 0::2] = words & 0xF
        nib[..., 1::2] = words >> 4
        vals = E2M1[nib]
    vals = vals * np.repeat(np.exp2(scales.astype(np.float64) - 127.0), 8, axis=1)[..., None]
    return vals.transpose(0, 1, 3, 2).reshape(g * 512, n)


def sigmoid(v):
    return 1.0 / (1.0 + np.exp(-v))


D, T, I, Q, U, Z, M = 512, 2048, 512, 128, 1024, 1024, 2048


def setup_inputs():
    n = np.random.standard_normal
    idx = np.random.permutation(T)[:I]
    idx2 = np.random.permutation(U)[:I]
    idx3 = np.random.permutation(Z)[:I]
    idx4 = np.random.permutation(M)[:I]
    fd = mx_kscale(D)
    keysp = pack_weight(n((D, T)) / fd[:, None], "e4m3")
    return {
        "query": (n((D, Q)) * 0.6 / np.sqrt(D) * fd[:, None]).astype(np.float32),
        "query2": (n((D, Q)) * 0.6 / np.sqrt(D) * fd[:, None]).astype(np.float32),
        "query3": (n((D, Q)) * 0.6 / np.sqrt(D) * fd[:, None]).astype(np.float32),
        "keys_words": keysp[0],
        "keys_scales": keysp[1],
        "notes": (n((D, U)) / fd[:, None]).astype(np.float32),
        "pages": (n((D, Z)) / fd[:, None]).astype(np.float32),
        "old": (np.random.uniform(0.0, 2.0, (Q, M))).astype(np.float32),
        "fade": (np.random.uniform(0.3, 0.9, (Q, 1))).astype(np.float32),
        "offs": striped(idx),
        "offs2": striped(idx2),
        "offs3": striped(idx3),
        "offs4": striped(idx4),
    }


def reference(query, query2, query3, keys_words, keys_scales, notes, pages, old, fade, offs, offs2, offs3, offs4):
    idx = unstriped(offs)
    idx2 = unstriped(offs2)
    idx3 = unstriped(offs3)
    idx4 = unstriped(offs4)
    keysu = unpack_weight(keys_words, keys_scales, "e4m3")
    queryq = mxq(f64(query), 0, "e4m3")
    keysidxg = keysu[:, idx]
    query2q = mxq(f64(query2), 0, "e4m3")
    notesidx2q = mxq(f64(notes)[:, idx2], 0, "e4m3")
    query3q = mxq(f64(query3), 0, "e4m3")
    pagesidx3q = mxq(f64(pages)[:, idx3], 0, "e4m3")
    s = queryq.T @ keysidxg + query2q.T @ notesidx2q + query3q.T @ pagesidx3q
    w = sigmoid(s)
    ws = w * 2.0
    wf = np.zeros((Q, M))
    wf[:, idx4] = ws
    y = f64(old) * f64(fade) + wf
    return y

@@ -1,0 +1,170 @@
+from contextlib import ExitStack
+
+import concourse.mybir as mybir
+
+D, T, I, Q, U, M = 512, 2048, 512, 128, 1024, 2048
+FLOPS = 3 * 2 * D * Q * I
+
+F32 = mybir.dt.float32
+BF16 = mybir.dt.bfloat16
+I32 = mybir.dt.int32
+U32 = mybir.dt.uint32
+U16 = mybir.dt.uint16
+U8 = mybir.dt.uint8
+FP8X4 = mybir.dt.float8_e4m3fn_x4
+ACT = mybir.ActivationFunctionType
+ALU = mybir.AluOpType
+
+P = 128
+PACK = 4
+SLOT_CHUNKS = ((0, 128), (128, 256), (256, 512))
+SCATTER_CHUNKS = ((0, 128), (128, 512))
+OUT_CHUNKS = ((0, 256), (256, 768), (768, 1280), (1280, 1792), (1792, 2048))
+
+
+def list_slice(offsets, lo, hi):
+    return offsets[:, lo // 16 : hi // 16]
+
+
+def tile_attend_threesources_counts_lean_kernel(
+    tc, query, query2, query3, keys_words, keys_scales, notes, pages, old, fade, offs, offs2, offs3, offs4, out
+):
+    nc = tc.nc
+    with ExitStack() as ctx:
+        keep = ctx.enter_context(tc.tile_pool(name="keep", bufs=1))
+        psum = ctx.enter_context(tc.psum_pool(name="psum", bufs=1))
+
+        def sb(name, shape, dtype):
+            return keep.tile(shape, dtype, name=name, align_bytes=64)
+
+        list1, list2, list3, list4 = (sb("list%d" % n, [P, I // 16], U16) for n in (1, 2, 3, 4))
+        note_planes = [sb("note_plane%d" % t, [P, U], F32) for t in range(PACK)]
+        page_planes = [sb("page_plane%d" % t, [P, U], F32) for t in range(PACK)]
+        key_words = sb("key_words", [P, T], I32)
+        key_scales = sb("key_scales", [P, T], U8)
+        q_raw = [sb("q_raw%d" % n, [P, PACK, Q], F32) for n in range(3)]
+        old_sb = sb("old_sb", [P, M], F32)
+        fade_sb = sb("fade_sb", [P, 1], F32)
+        placed = sb("placed", [P, M], F32)
+
+        notes_by_plane = notes.rearrange("(p t) u -> p t u", t=PACK)
+        pages_by_plane = pages.rearrange("(p t) u -> p t u", t=PACK)
+
+        nc.vector.memset(key_scales[:].bitcast(I32), 0)
+        nc.vector.memset(placed[:], 0.0)
+        ones = sb("ones", [P, 384], F32)
+        zeros = sb("zeros", [P, 384], F32)
+        nc.gpsimd.memset(zeros[:], 0.0)
+        nc.scalar.activation(ones[:], zeros[:], ACT.Copy, bias=1.0)
+
+        def load_scales(quad):
+            nc.sync.dma_start(
+                out=key_scales[32 * quad : 32 * quad + 4, :].bitcast(I32),
+                in_=keys_scales[0, 4 * quad : 4 * quad + 4, :].bitcast(I32),
+            )
+
+        nc.sync.dma_start(out=note_planes[0][:], in_=notes_by_plane[:, 0, :])
+        nc.sync.dma_start(list2[:], offs2)
+        nc.sync.dma_start(out=note_planes[1][:], in_=notes_by_plane[:, 1, :])
+        nc.sync.dma_start(list1[:], offs)
+        for quad in range(2):
+            load_scales(quad)
+        nc.sync.dma_start(out=note_planes[2][:], in_=notes_by_plane[:, 2, :])
+        for quad in range(2, 4):
+            load_scales(quad)
+        nc.sync.dma_start(out=note_planes[3][:], in_=notes_by_plane[:, 3, :])
+        nc.sync.dma_start(out=page_planes[0][:], in_=pages_by_plane[:, 0, :])
+        nc.sync.dma_start(list3[:], offs3)
+        for t in range(1, PACK):
+            nc.sync.dma_start(out=page_planes[t][:], in_=pages_by_plane[:, t, :])
+        for n, src in enumerate((query2, query3, query)):
+            nc.sync.dma_start(out=q_raw[n][:], in_=src.rearrange("(p t) q -> p t q", t=PACK))
+        nc.sync.dma_start(out=key_words[:], in_=keys_words[0].rearrange("p n t -> p (n t)").bitcast(I32))
+        nc.sync.dma_start(list4[:], offs4)
+        nc.sync.dma_start(out=fade_sb[:], in_=fade)
+        nc.sync.dma_start(out=old_sb[:], in_=old)
+
+        def gather_vector(dst, plane, offsets):
+            nc.vector.tensor_copy(dst, plane[:].indirect(offsets))
+
+        def gather_scalar(dst, plane, offsets):
+            nc.scalar.activation(dst, plane[:].indirect(offsets), ACT.Copy)
+
+        note_picked = sb("note_picked", [P, PACK, I], BF16)
+        page_picked = sb("page_picked", [P, PACK, I], BF16)
+        note_woven = sb("note_woven", [P, I, PACK], BF16)
+        page_woven = sb("page_woven", [P, I, PACK], BF16)
+        note_codes = sb("note_codes", [P, I], U32)
+        page_codes = sb("page_codes", [P, I], U32)
+        note_scales = sb("note_scales", [P, I], U8)
+        page_scales = sb("page_scales", [P, I], U8)
+        picked_scales = sb("picked_scales", [P, I], U8)
+        picked_words = [sb("picked_words%d" % c, [P, hi - lo], U32) for c, (lo, hi) in enumerate(SLOT_CHUNKS)]
+        q_woven = [sb("q_woven%d" % n, [P, Q, PACK], BF16) for n in range(3)]
+        q_codes = [sb("q_codes%d" % n, [P, Q], U32) for n in range(3)]
+        q_scales = [sb("q_scales%d" % n, [P, Q], U8) for n in range(3)]
+        weights = sb("weights", [P, I], F32)
+        result = [sb("result%d" % c, [P, hi - lo], F32) for c, (lo, hi) in enumerate(OUT_CHUNKS)]
+        banks = [psum.tile([P, hi - lo], F32, name="bank%d" % c) for c, (lo, hi) in enumerate(SLOT_CHUNKS)]
+
+        def weave(woven, picked):
+            nc.vector.tensor_copy(out=woven[:], in_=picked[:].rearrange("p t i -> p i t"))
+
+        def quantise(codes, scales, woven):
+            nc.vector.quantize_mx(out=codes.bitcast(FP8X4), scales=scales, in_=woven)
+
+        half = I // 2
+        nc.vector.tensor_copy(picked_scales[:], key_scales[:].indirect(list1[:]))
+        for t in range(PACK - 1):
+            gather_scalar(note_picked[:, t, :], note_planes[t], list2[:])
+        gather_vector(note_picked[:, 3, :half], note_planes[3], list_slice(list2, 0, half))
+        gather_scalar(note_picked[:, 3, half:], note_planes[3], list_slice(list2, half, I))
+        weave(note_woven, note_picked)
+        quantise(note_codes[:], note_scales[:], note_woven[:].rearrange("p i t -> p (i t)"))
+
+        gather_scalar(page_picked[:, 0, :], page_planes[0], list3[:])
+        gather_scalar(page_picked[:, 1, :], page_planes[1], list3[:])
+        gather_vector(page_picked[:, 2, :], page_planes[2], list3[:])
+        gather_vector(page_picked[:, 3, :half], page_planes[3], list_slice(list3, 0, half))
+        gather_scalar(page_picked[:, 3, half:], page_planes[3], list_slice(list3, half, I))
+        halves = ((0, half), (half, I))
+        for lo, hi in halves:
+            nc.vector.tensor_copy(out=page_woven[:, lo:hi, :], in_=page_picked[:, :, lo:hi].rearrange("p t i -> p i t"))
+        for lo, hi in halves:
+            quantise(page_codes[:, lo:hi], page_scales[:, lo:hi], page_woven[:, lo:hi, :].rearrange("p i t -> p (i t)"))
+
+        for n in range(3):
+            nc.scalar.copy(out=q_woven[n][:], in_=q_raw[n][:].rearrange("p t q -> p q t"))
+            quantise(q_codes[n][:], q_scales[n][:], q_woven[n][:].rearrange("p q t -> p (q t)"))
+
+        def product(c, n, codes, scales, start, stop):
+            nc.tensor.matmul_mx(
+                out=banks[c][:],
+                lhsT=q_codes[n][:].bitcast(FP8X4),
+                lhsT_scale=q_scales[n][:],
+                rhs=codes.bitcast(FP8X4),
+                rhs_scale=scales,
+                start=start,
+                stop=stop,
+            )
+
+        for c, (lo, hi) in enumerate(SLOT_CHUNKS):
+            product(c, 0, note_codes[:, lo:hi], note_scales[:, lo:hi], True, False)
+        for c, (lo, hi) in enumerate(SLOT_CHUNKS):
+            product(c, 1, page_codes[:, lo:hi], page_scales[:, lo:hi], False, False)
+        for c, (lo, hi) in enumerate(SLOT_CHUNKS):
+            nc.vector.tensor_copy(picked_words[c][:], key_words[:].bitcast(U32).indirect(list_slice(list1, lo, hi)))
+            product(c, 2, picked_words[c][:], picked_scales[:, lo:hi], False, True)
+            nc.scalar.activation(weights[:, lo:hi], banks[c][:], ACT.Tanh, scale=0.5)
+
+        for lo, hi in SCATTER_CHUNKS:
+            nc.vector.tensor_tensor(
+                placed[:].indirect(list_slice(list4, lo, hi)), weights[:, lo:hi], ones[:, : hi - lo], ALU.add
+            )
+
+        for c, (lo, hi) in enumerate(OUT_CHUNKS):
+            nc.vector.scalar_tensor_tensor(
+                out=result[c][:], in0=old_sb[:, lo:hi], scalar=fade_sb[:, 0:1], in1=placed[:, lo:hi],
+                op0=ALU.mult, op1=ALU.add,
+            )
+            nc.sync.dma_start(out=out[:, lo:hi], in_=result[c][:])

@@ -17,9 +17,9 @@ ALU = mybir.AluOpType
 
 P = 128
 PACK = 4
-SLOT_CHUNKS = ((0, 128), (128, 256), (256, 512))
+SLOT_CHUNKS = ((0, 128), (128, 384), (384, 512))
 SCATTER_CHUNKS = ((0, 128), (128, 512))
-OUT_CHUNKS = ((0, 256), (256, 768), (768, 1280), (1280, 1792), (1792, 2048))
+OUT_CHUNKS = ((0, 128), (128, 512), (512, 1024), (1024, 1536), (1536, 2048))
 
 
 def list_slice(offsets, lo, hi):
@@ -50,31 +50,25 @@ def tile_attend_threesources_counts_lean_kernel(
         notes_by_plane = notes.rearrange("(p t) u -> p t u", t=PACK)
         pages_by_plane = pages.rearrange("(p t) u -> p t u", t=PACK)
 
-        nc.vector.memset(key_scales[:].bitcast(I32), 0)
-        nc.vector.memset(placed[:], 0.0)
         ones = sb("ones", [P, 384], F32)
         zeros = sb("zeros", [P, 384], F32)
-        nc.gpsimd.memset(zeros[:], 0.0)
+        nc.vector.memset(zeros[:], 0.0)
         nc.scalar.activation(ones[:], zeros[:], ACT.Copy, bias=1.0)
-
-        def load_scales(quad):
-            nc.sync.dma_start(
-                out=key_scales[32 * quad : 32 * quad + 4, :].bitcast(I32),
-                in_=keys_scales[0, 4 * quad : 4 * quad + 4, :].bitcast(I32),
+        nc.vector.memset(placed[:], 0.0)
+        nc.gpsimd.memset(key_scales[:].bitcast(I32), 0)
+        for r in range(4):
+            nc.gpsimd.dma_start(
+                out=key_scales[r:P:32, :].bitcast(I32),
+                in_=keys_scales[0, r:16:4, :].bitcast(I32),
             )
 
         nc.sync.dma_start(out=note_planes[0][:], in_=notes_by_plane[:, 0, :])
         nc.sync.dma_start(list2[:], offs2)
-        nc.sync.dma_start(out=note_planes[1][:], in_=notes_by_plane[:, 1, :])
-        nc.sync.dma_start(list1[:], offs)
-        for quad in range(2):
-            load_scales(quad)
-        nc.sync.dma_start(out=note_planes[2][:], in_=notes_by_plane[:, 2, :])
-        for quad in range(2, 4):
-            load_scales(quad)
-        nc.sync.dma_start(out=note_planes[3][:], in_=notes_by_plane[:, 3, :])
-        nc.sync.dma_start(out=page_planes[0][:], in_=pages_by_plane[:, 0, :])
+        for t in range(1, PACK):
+            nc.sync.dma_start(out=note_planes[t][:], in_=notes_by_plane[:, t, :])
         nc.sync.dma_start(list3[:], offs3)
+        nc.sync.dma_start(out=page_planes[0][:], in_=pages_by_plane[:, 0, :])
+        nc.sync.dma_start(list1[:], offs)
         for t in range(1, PACK):
             nc.sync.dma_start(out=page_planes[t][:], in_=pages_by_plane[:, t, :])
         for n, src in enumerate((query2, query3, query)):
@@ -90,7 +84,7 @@ def tile_attend_threesources_counts_lean_kernel(
         def gather_scalar(dst, plane, offsets):
             nc.scalar.activation(dst, plane[:].indirect(offsets), ACT.Copy)
 
-        note_picked = sb("note_picked", [P, PACK, I], BF16)
+        note_picked = keep.tile([P, PACK, I], BF16, name="note_picked", tag="reused", align_bytes=64)
         page_picked = sb("page_picked", [P, PACK, I], BF16)
         note_woven = sb("note_woven", [P, I, PACK], BF16)
         page_woven = sb("page_woven", [P, I, PACK], BF16)
@@ -98,7 +92,6 @@ def tile_attend_threesources_counts_lean_kernel(
         page_codes = sb("page_codes", [P, I], U32)
         note_scales = sb("note_scales", [P, I], U8)
         page_scales = sb("page_scales", [P, I], U8)
-        picked_scales = sb("picked_scales", [P, I], U8)
         picked_words = [sb("picked_words%d" % c, [P, hi - lo], U32) for c, (lo, hi) in enumerate(SLOT_CHUNKS)]
         q_woven = [sb("q_woven%d" % n, [P, Q, PACK], BF16) for n in range(3)]
         q_codes = [sb("q_codes%d" % n, [P, Q], U32) for n in range(3)]
@@ -114,14 +107,16 @@ def tile_attend_threesources_counts_lean_kernel(
             nc.vector.quantize_mx(out=codes.bitcast(FP8X4), scales=scales, in_=woven)
 
         half = I // 2
-        nc.vector.tensor_copy(picked_scales[:], key_scales[:].indirect(list1[:]))
-        for t in range(PACK - 1):
-            gather_scalar(note_picked[:, t, :], note_planes[t], list2[:])
+        gather_scalar(note_picked[:, 0, :], note_planes[0], list2[:])
+        gather_vector(note_picked[:, 1, :], note_planes[1], list2[:])
+        gather_scalar(note_picked[:, 2, :], note_planes[2], list2[:])
         gather_vector(note_picked[:, 3, :half], note_planes[3], list_slice(list2, 0, half))
         gather_scalar(note_picked[:, 3, half:], note_planes[3], list_slice(list2, half, I))
         weave(note_woven, note_picked)
         quantise(note_codes[:], note_scales[:], note_woven[:].rearrange("p i t -> p (i t)"))
 
+        picked_scales = keep.tile([P, I], U8, name="picked_scales", tag="reused", align_bytes=64)
+        nc.vector.tensor_copy(picked_scales[:], key_scales[:].indirect(list1[:]))
         gather_scalar(page_picked[:, 0, :], page_planes[0], list3[:])
         gather_scalar(page_picked[:, 1, :], page_planes[1], list3[:])
         gather_vector(page_picked[:, 2, :], page_planes[2], list3[:])

@@ -38,8 +38,8 @@ def tile_attend_threesources_counts_lean_kernel(
             return keep.tile(shape, dtype, name=name, align_bytes=64)
 
         list1, list2, list3, list4 = (sb("list%d" % n, [P, I // 16], U16) for n in (1, 2, 3, 4))
-        note_planes = [sb("note_plane%d" % t, [P, U], F32) for t in range(PACK)]
-        page_planes = [sb("page_plane%d" % t, [P, U], F32) for t in range(PACK)]
+        note_pairs = [sb("note_pair%d" % h, [P, 2, U], F32) for h in range(2)]
+        page_pairs = [sb("page_pair%d" % h, [P, 2, U], F32) for h in range(2)]
         key_words = sb("key_words", [P, T], I32)
         key_scales = sb("key_scales", [P, T], U8)
         q_raw = [sb("q_raw%d" % n, [P, PACK, Q], F32) for n in range(3)]
@@ -56,21 +56,20 @@ def tile_attend_threesources_counts_lean_kernel(
         nc.scalar.activation(ones[:], zeros[:], ACT.Copy, bias=1.0)
         nc.vector.memset(placed[:], 0.0)
         nc.gpsimd.memset(key_scales[:].bitcast(I32), 0)
+
+        nc.sync.dma_start(out=note_pairs[0][:], in_=notes_by_plane[:, 0:2, :])
+        nc.sync.dma_start(list2[:], offs2)
         for r in range(4):
-            nc.gpsimd.dma_start(
+            nc.sync.dma_start(
                 out=key_scales[r:P:32, :].bitcast(I32),
                 in_=keys_scales[0, r:16:4, :].bitcast(I32),
             )
-
-        nc.sync.dma_start(out=note_planes[0][:], in_=notes_by_plane[:, 0, :])
-        nc.sync.dma_start(list2[:], offs2)
-        for t in range(1, PACK):
-            nc.sync.dma_start(out=note_planes[t][:], in_=notes_by_plane[:, t, :])
-        nc.sync.dma_start(list3[:], offs3)
-        nc.sync.dma_start(out=page_planes[0][:], in_=pages_by_plane[:, 0, :])
         nc.sync.dma_start(list1[:], offs)
-        for t in range(1, PACK):
-            nc.sync.dma_start(out=page_planes[t][:], in_=pages_by_plane[:, t, :])
+        nc.sync.dma_start(out=note_pairs[1][:], in_=notes_by_plane[:, 2:4, :])
+        nc.sync.dma_start(list3[:], offs3)
+        nc.sync.dma_start(out=page_pairs[0][:], in_=pages_by_plane[:, 0:2, :])
+        for t in (2, 3):
+            nc.sync.dma_start(out=page_pairs[1][:, t - 2, :], in_=pages_by_plane[:, t, :])
         for n, src in enumerate((query2, query3, query)):
             nc.sync.dma_start(out=q_raw[n][:], in_=src.rearrange("(p t) q -> p t q", t=PACK))
         nc.sync.dma_start(out=key_words[:], in_=keys_words[0].rearrange("p n t -> p (n t)").bitcast(I32))
@@ -79,13 +78,14 @@ def tile_attend_threesources_counts_lean_kernel(
         nc.sync.dma_start(out=old_sb[:], in_=old)
 
         def gather_vector(dst, plane, offsets):
-            nc.vector.tensor_copy(dst, plane[:].indirect(offsets))
+            nc.vector.tensor_copy(dst, plane.indirect(offsets))
 
         def gather_scalar(dst, plane, offsets):
-            nc.scalar.activation(dst, plane[:].indirect(offsets), ACT.Copy)
+            nc.scalar.activation(dst, plane.indirect(offsets), ACT.Copy)
 
-        note_picked = keep.tile([P, PACK, I], BF16, name="note_picked", tag="reused", align_bytes=64)
-        page_picked = sb("page_picked", [P, PACK, I], BF16)
+        note_picked = sb("note_picked", [P, PACK, I], F32)
+        page_picked = sb("page_picked", [P, PACK, I], F32)
+        picked_scales = sb("picked_scales", [P, I], U8)
         note_woven = sb("note_woven", [P, I, PACK], BF16)
         page_woven = sb("page_woven", [P, I, PACK], BF16)
         note_codes = sb("note_codes", [P, I], U32)
@@ -100,36 +100,35 @@ def tile_attend_threesources_counts_lean_kernel(
         result = [sb("result%d" % c, [P, hi - lo], F32) for c, (lo, hi) in enumerate(OUT_CHUNKS)]
         banks = [psum.tile([P, hi - lo], F32, name="bank%d" % c) for c, (lo, hi) in enumerate(SLOT_CHUNKS)]
 
-        def weave(woven, picked):
-            nc.vector.tensor_copy(out=woven[:], in_=picked[:].rearrange("p t i -> p i t"))
+        def weave(copy, woven, picked):
+            copy(out=woven.rearrange("p (c i) t -> p c t i", i=4), in_=picked.rearrange("p t (c i) -> p c t i", i=4))
 
         def quantise(codes, scales, woven):
             nc.vector.quantize_mx(out=codes.bitcast(FP8X4), scales=scales, in_=woven)
 
         half = I // 2
-        gather_scalar(note_picked[:, 0, :], note_planes[0], list2[:])
-        gather_vector(note_picked[:, 1, :], note_planes[1], list2[:])
-        gather_scalar(note_picked[:, 2, :], note_planes[2], list2[:])
-        gather_vector(note_picked[:, 3, :half], note_planes[3], list_slice(list2, 0, half))
-        gather_scalar(note_picked[:, 3, half:], note_planes[3], list_slice(list2, half, I))
-        weave(note_woven, note_picked)
-        quantise(note_codes[:], note_scales[:], note_woven[:].rearrange("p i t -> p (i t)"))
+        def gather_pair(picked, pairs, h, offsets):
+            gather_scalar(picked[:, 2 * h, :], pairs[h][:, 0, :], offsets[:])
+            gather_vector(picked[:, 2 * h + 1, :], pairs[h][:, 1, :], offsets[:])
 
-        picked_scales = keep.tile([P, I], U8, name="picked_scales", tag="reused", align_bytes=64)
+        gather_pair(note_picked, note_pairs, 0, list2)
         nc.vector.tensor_copy(picked_scales[:], key_scales[:].indirect(list1[:]))
-        gather_scalar(page_picked[:, 0, :], page_planes[0], list3[:])
-        gather_scalar(page_picked[:, 1, :], page_planes[1], list3[:])
-        gather_vector(page_picked[:, 2, :], page_planes[2], list3[:])
-        gather_vector(page_picked[:, 3, :half], page_planes[3], list_slice(list3, 0, half))
-        gather_scalar(page_picked[:, 3, half:], page_planes[3], list_slice(list3, half, I))
+        gather_pair(note_picked, note_pairs, 1, list2)
+        weave(nc.vector.tensor_copy, note_woven[:], note_picked[:])
+        quantise(note_codes[:], note_scales[:], note_woven[:].rearrange("p i t -> p (i t)"))
+        gather_scalar(page_picked[:, 0, :], page_pairs[0][:, 0, :], list3[:])
+        gather_scalar(page_picked[:, 1, :], page_pairs[0][:, 1, :], list3[:])
+        gather_vector(page_picked[:, 2, :], page_pairs[1][:, 0, :], list3[:])
+        gather_vector(page_picked[:, 3, :half], page_pairs[1][:, 1, :], list_slice(list3, 0, half))
+        gather_scalar(page_picked[:, 3, half:], page_pairs[1][:, 1, :], list_slice(list3, half, I))
         halves = ((0, half), (half, I))
         for lo, hi in halves:
-            nc.vector.tensor_copy(out=page_woven[:, lo:hi, :], in_=page_picked[:, :, lo:hi].rearrange("p t i -> p i t"))
+            weave(nc.vector.tensor_copy, page_woven[:, lo:hi, :], page_picked[:, :, lo:hi])
         for lo, hi in halves:
             quantise(page_codes[:, lo:hi], page_scales[:, lo:hi], page_woven[:, lo:hi, :].rearrange("p i t -> p (i t)"))
 
         for n in range(3):
-            nc.scalar.copy(out=q_woven[n][:], in_=q_raw[n][:].rearrange("p t q -> p q t"))
+            weave(nc.scalar.copy, q_woven[n][:], q_raw[n][:])
             quantise(q_codes[n][:], q_scales[n][:], q_woven[n][:].rearrange("p q t -> p (q t)"))
 
         def product(c, n, codes, scales, start, stop):

@@ -106,7 +106,7 @@ def tile_attend_threesources_counts_lean_kernel(
         def quantise(codes, scales, woven):
             nc.vector.quantize_mx(out=codes.bitcast(FP8X4), scales=scales, in_=woven)
 
-        half = I // 2
+        half = 128
         def gather_pair(picked, pairs, h, offsets):
             gather_scalar(picked[:, 2 * h, :], pairs[h][:, 0, :], offsets[:])
             gather_vector(picked[:, 2 * h + 1, :], pairs[h][:, 1, :], offsets[:])
@@ -114,7 +114,8 @@ def tile_attend_threesources_counts_lean_kernel(
         gather_pair(note_picked, note_pairs, 0, list2)
         nc.vector.tensor_copy(picked_scales[:], key_scales[:].indirect(list1[:]))
         gather_pair(note_picked, note_pairs, 1, list2)
-        weave(nc.vector.tensor_copy, note_woven[:], note_picked[:])
+        weave(nc.vector.tensor_copy, note_woven[:, :384, :], note_picked[:, :, :384])
+        weave(nc.scalar.copy, note_woven[:, 384:, :], note_picked[:, :, 384:])
         quantise(note_codes[:], note_scales[:], note_woven[:].rearrange("p i t -> p (i t)"))
         gather_scalar(page_picked[:, 0, :], page_pairs[0][:, 0, :], list3[:])
         gather_scalar(page_picked[:, 1, :], page_pairs[0][:, 1, :], list3[:])

from contextlib import ExitStack

import concourse.mybir as mybir

D, T, I, Q, U, M = 512, 2048, 512, 128, 1024, 2048
FLOPS = 3 * 2 * D * Q * I

F32 = mybir.dt.float32
BF16 = mybir.dt.bfloat16
I32 = mybir.dt.int32
U32 = mybir.dt.uint32
U16 = mybir.dt.uint16
U8 = mybir.dt.uint8
FP8X4 = mybir.dt.float8_e4m3fn_x4
ACT = mybir.ActivationFunctionType
ALU = mybir.AluOpType

P = 128
PACK = 4
SLOT_CHUNKS = ((0, 128), (128, 384), (384, 512))
SCATTER_CHUNKS = ((0, 128), (128, 512))
OUT_CHUNKS = ((0, 128), (128, 512), (512, 1024), (1024, 1536), (1536, 2048))


def list_slice(offsets, lo, hi):
    return offsets[:, lo // 16 : hi // 16]


def tile_attend_threesources_counts_lean_kernel(
    tc, query, query2, query3, keys_words, keys_scales, notes, pages, old, fade, offs, offs2, offs3, offs4, out
):
    nc = tc.nc
    with ExitStack() as ctx:
        keep = ctx.enter_context(tc.tile_pool(name="keep", bufs=1))
        psum = ctx.enter_context(tc.psum_pool(name="psum", bufs=1))

        def sb(name, shape, dtype):
            return keep.tile(shape, dtype, name=name, align_bytes=64)

        list1, list2, list3, list4 = (sb("list%d" % n, [P, I // 16], U16) for n in (1, 2, 3, 4))
        note_pairs = [sb("note_pair%d" % h, [P, 2, U], F32) for h in range(2)]
        page_pairs = [sb("page_pair%d" % h, [P, 2, U], F32) for h in range(2)]
        key_words = sb("key_words", [P, T], I32)
        key_scales = sb("key_scales", [P, T], U8)
        q_raw = [sb("q_raw%d" % n, [P, PACK, Q], F32) for n in range(3)]
        old_sb = sb("old_sb", [P, M], F32)
        fade_sb = sb("fade_sb", [P, 1], F32)
        placed = sb("placed", [P, M], F32)

        notes_by_plane = notes.rearrange("(p t) u -> p t u", t=PACK)
        pages_by_plane = pages.rearrange("(p t) u -> p t u", t=PACK)

        ones = sb("ones", [P, 384], F32)
        zeros = sb("zeros", [P, 384], F32)
        nc.vector.memset(zeros[:], 0.0)
        nc.scalar.activation(ones[:], zeros[:], ACT.Copy, bias=1.0)
        nc.vector.memset(placed[:], 0.0)
        nc.gpsimd.memset(key_scales[:].bitcast(I32), 0)

        nc.sync.dma_start(out=note_pairs[0][:], in_=notes_by_plane[:, 0:2, :])
        nc.sync.dma_start(list2[:], offs2)
        for r in range(4):
            nc.sync.dma_start(
                out=key_scales[r:P:32, :].bitcast(I32),
                in_=keys_scales[0, r:16:4, :].bitcast(I32),
            )
        nc.sync.dma_start(list1[:], offs)
        nc.sync.dma_start(out=note_pairs[1][:], in_=notes_by_plane[:, 2:4, :])
        nc.sync.dma_start(list3[:], offs3)
        nc.sync.dma_start(out=page_pairs[0][:], in_=pages_by_plane[:, 0:2, :])
        for t in (2, 3):
            nc.sync.dma_start(out=page_pairs[1][:, t - 2, :], in_=pages_by_plane[:, t, :])
        for n, src in enumerate((query2, query3, query)):
            nc.sync.dma_start(out=q_raw[n][:], in_=src.rearrange("(p t) q -> p t q", t=PACK))
        nc.sync.dma_start(out=key_words[:], in_=keys_words[0].rearrange("p n t -> p (n t)").bitcast(I32))
        nc.sync.dma_start(list4[:], offs4)
        nc.sync.dma_start(out=fade_sb[:], in_=fade)
        nc.sync.dma_start(out=old_sb[:], in_=old)

        def gather_vector(dst, plane, offsets):
            nc.vector.tensor_copy(dst, plane.indirect(offsets))

        def gather_scalar(dst, plane, offsets):
            nc.scalar.activation(dst, plane.indirect(offsets), ACT.Copy)

        note_picked = sb("note_picked", [P, PACK, I], F32)
        page_picked = sb("page_picked", [P, PACK, I], F32)
        picked_scales = sb("picked_scales", [P, I], U8)
        note_woven = sb("note_woven", [P, I, PACK], BF16)
        page_woven = sb("page_woven", [P, I, PACK], BF16)
        note_codes = sb("note_codes", [P, I], U32)
        page_codes = sb("page_codes", [P, I], U32)
        note_scales = sb("note_scales", [P, I], U8)
        page_scales = sb("page_scales", [P, I], U8)
        picked_words = [sb("picked_words%d" % c, [P, hi - lo], U32) for c, (lo, hi) in enumerate(SLOT_CHUNKS)]
        q_woven = [sb("q_woven%d" % n, [P, Q, PACK], BF16) for n in range(3)]
        q_codes = [sb("q_codes%d" % n, [P, Q], U32) for n in range(3)]
        q_scales = [sb("q_scales%d" % n, [P, Q], U8) for n in range(3)]
        weights = sb("weights", [P, I], F32)
        result = [sb("result%d" % c, [P, hi - lo], F32) for c, (lo, hi) in enumerate(OUT_CHUNKS)]
        banks = [psum.tile([P, hi - lo], F32, name="bank%d" % c) for c, (lo, hi) in enumerate(SLOT_CHUNKS)]

        def weave(copy, woven, picked):
            copy(out=woven.rearrange("p (c i) t -> p c t i", i=4), in_=picked.rearrange("p t (c i) -> p c t i", i=4))

        def quantise(codes, scales, woven):
            nc.vector.quantize_mx(out=codes.bitcast(FP8X4), scales=scales, in_=woven)

        half = 128
        def gather_pair(picked, pairs, h, offsets):
            gather_scalar(picked[:, 2 * h, :], pairs[h][:, 0, :], offsets[:])
            gather_vector(picked[:, 2 * h + 1, :], pairs[h][:, 1, :], offsets[:])

        gather_pair(note_picked, note_pairs, 0, list2)
        nc.vector.tensor_copy(picked_scales[:], key_scales[:].indirect(list1[:]))
        gather_pair(note_picked, note_pairs, 1, list2)
        weave(nc.vector.tensor_copy, note_woven[:, :384, :], note_picked[:, :, :384])
        weave(nc.scalar.copy, note_woven[:, 384:, :], note_picked[:, :, 384:])
        quantise(note_codes[:], note_scales[:], note_woven[:].rearrange("p i t -> p (i t)"))
        gather_scalar(page_picked[:, 0, :], page_pairs[0][:, 0, :], list3[:])
        gather_scalar(page_picked[:, 1, :], page_pairs[0][:, 1, :], list3[:])
        gather_vector(page_picked[:, 2, :], page_pairs[1][:, 0, :], list3[:])
        gather_vector(page_picked[:, 3, :half], page_pairs[1][:, 1, :], list_slice(list3, 0, half))
        gather_scalar(page_picked[:, 3, half:], page_pairs[1][:, 1, :], list_slice(list3, half, I))
        halves = ((0, half), (half, I))
        for lo, hi in halves:
            weave(nc.vector.tensor_copy, page_woven[:, lo:hi, :], page_picked[:, :, lo:hi])
        for lo, hi in halves:
            quantise(page_codes[:, lo:hi], page_scales[:, lo:hi], page_woven[:, lo:hi, :].rearrange("p i t -> p (i t)"))

        for n in range(3):
            weave(nc.scalar.copy, q_woven[n][:], q_raw[n][:])
            quantise(q_codes[n][:], q_scales[n][:], q_woven[n][:].rearrange("p q t -> p (q t)"))

        def product(c, n, codes, scales, start, stop):
            nc.tensor.matmul_mx(
                out=banks[c][:],
                lhsT=q_codes[n][:].bitcast(FP8X4),
                lhsT_scale=q_scales[n][:],
                rhs=codes.bitcast(FP8X4),
                rhs_scale=scales,
                start=start,
                stop=stop,
            )

        for c, (lo, hi) in enumerate(SLOT_CHUNKS):
            product(c, 0, note_codes[:, lo:hi], note_scales[:, lo:hi], True, False)
        for c, (lo, hi) in enumerate(SLOT_CHUNKS):
            product(c, 1, page_codes[:, lo:hi], page_scales[:, lo:hi], False, False)
        for c, (lo, hi) in enumerate(SLOT_CHUNKS):
            nc.vector.tensor_copy(picked_words[c][:], key_words[:].bitcast(U32).indirect(list_slice(list1, lo, hi)))
            product(c, 2, picked_words[c][:], picked_scales[:, lo:hi], False, True)
            nc.scalar.activation(weights[:, lo:hi], banks[c][:], ACT.Tanh, scale=0.5)

        for lo, hi in SCATTER_CHUNKS:
            nc.vector.tensor_tensor(
                placed[:].indirect(list_slice(list4, lo, hi)), weights[:, lo:hi], ones[:, : hi - lo], ALU.add
            )

        for c, (lo, hi) in enumerate(OUT_CHUNKS):
            nc.vector.scalar_tensor_tensor(
                out=result[c][:], in0=old_sb[:, lo:hi], scalar=fade_sb[:, 0:1], in1=placed[:, lo:hi],
                op0=ALU.mult, op1=ALU.add,
            )
            nc.sync.dma_start(out=out[:, lo:hi], in_=result[c][:])
